import numpy as np
import ml_dtypes


def mxq(x, axis, fmt="e4m3"):
    dtype, down = {"e4m3": (ml_dtypes.float8_e4m3fn, 7), "e5m2": (ml_dtypes.float8_e5m2, 14)}[fmt]
    v = np.moveaxis(np.asarray(x, np.float32).astype(ml_dtypes.bfloat16).astype(np.float64), axis, -1)
    blocks = v.reshape(v.shape[:-1] + (-1, 32))
    amax = np.abs(blocks).max(-1, keepdims=True)
    byte = np.maximum(np.where(amax > 0, np.frexp(amax)[1] - 1 + 127, 0) - down, 1)
    scale = np.exp2(byte - 127.0)
    codes = (blocks / scale).astype(np.float32).astype(dtype).astype(np.float64)
    return np.moveaxis((codes * scale).reshape(v.shape), -1, axis)


WIDE = False


def mx_kscale(k):
    if not WIDE:
        return np.ones(k)
    levels = np.array([10, -10, 5, -5, 0])
    if k % 512:
        return np.exp2(np.random.permutation(np.resize(levels, k // 32))).repeat(32)
    a = np.empty((k // 512, 16))
    for p in range(k // 512):
        a[p, :8] = np.random.permutation(np.resize(levels, 8))
        for g in range(8):
            far = levels[np.abs(levels - a[p, g]) >= 10]
            a[p, g + 8] = far[np.random.randint(len(far))]
    return np.exp2(a.ravel()).repeat(32)


def f64(x):
    return np.asarray(x).astype(np.float64)


def striped(idx):
    return np.tile(np.asarray(idx).reshape(-1, 16).T, (8, 1)).astype(np.uint16)


def unstriped(offs):
    return offs[:16].T.reshape(-1).astype(np.int64)


E2M1 = np.array([0.0, 0.5, 1.0, 1.5, 2.0, 3.0, 4.0, 6.0, -0.0, -0.5, -1.0, -1.5, -2.0, -3.0, -4.0, -6.0])


def pack_weight(w, fmt):
    k, n = w.shape
    w = f64(np.asarray(w, np.float32).astype(ml_dtypes.bfloat16)).reshape(k // 32, 32, n)
    amax = np.abs(w).max(1)
    if fmt == "e4m3":
        byte = np.frexp(amax)[1] - 1 + 127 - 7
    else:
        mant, ex = np.frexp(amax / 6.0)
        byte = np.where(mant > 0.5, ex, ex - 1) + 127
    byte = np.clip(np.where(amax > 0, byte, 1), 1, 254)
    scaled = (w * np.exp2(127.0 - byte)[:, None, :]).reshape(k, n).astype(np.float32)
    by_word = np.ascontiguousarray(scaled.reshape(k // 512, 128, 4, n).transpose(0, 1, 3, 2))
    if fmt == "e4m3":
        words = by_word.astype(ml_dtypes.float8_e4m3fn).view(np.uint8)
    else:
        c = by_word.astype(ml_dtypes.float4_e2m1fn).view(np.uint8) & 0xF
        words = (c[..., 0::2] | (c[..., 1::2] << 4)).reshape(k // 512, 128, 2 * n)
    return np.ascontiguousarray(words), np.ascontiguousarray(byte.astype(np.uint8).reshape(k // 512, 16, n))


def unpack_weight(words, scales, fmt):
    g, _, n = scales.shape
    words = np.ascontiguousarray(words).reshape(g, 128, n, -1)
    if fmt == "e4m3":
        vals = words.view(ml_dtypes.float8_e4m3fn).astype(np.float64)
    else:
        nib = np.empty((g, 128, n, 4), np.uint8)
        nib[..., 0::2] = words & 0xF
        nib[..., 1::2] = words >> 4
        vals = E2M1[nib]
    vals = vals * np.repeat(np.exp2(scales.astype(np.float64) - 127.0), 8, axis=1)[..., None]
    return vals.transpose(0, 1, 3, 2).reshape(g * 512, n)


D, T, I, J, U, H, M = 512, 2048, 512, 512, 1024, 512, 1024


def setup_inputs():
    n = np.random.standard_normal
    idx = np.random.permutation(T)[:I]
    idx2 = np.random.permutation(U)[:J]
    idx3 = np.random.permutation(M)[:J]
    fd = mx_kscale(D)
    fh = mx_kscale(H)
    keysp = pack_weight(n((D, T)) / fd[:, None], "e4m3")
    return {
        "keys_words": keysp[0],
        "keys_scales": keysp[1],
        "wk": (n((D, H)) * 1.0 / np.sqrt(D) * fd[:, None] * fh).astype(np.float32),
        "notes": (n((H, U)) * 1.0 / np.sqrt(H) / fh[:, None]).astype(np.float32),
        "old": (1.0 * n((I, M))).astype(np.float32),
        "fade": (np.random.uniform(0.3, 0.9, (I, 1))).astype(np.float32),
        "offs": striped(idx),
        "offs2": striped(idx2),
        "offs3": striped(idx3),
    }


def reference(keys_words, keys_scales, wk, notes, old, fade, offs, offs2, offs3):
    idx = unstriped(offs)
    idx2 = unstriped(offs2)
    idx3 = unstriped(offs3)
    keysu = unpack_weight(keys_words, keys_scales, "e4m3")
    wkq = mxq(f64(wk), 0, "e4m3")
    keysidxg = keysu[:, idx]
    kp = wkq.T @ keysidxg
    kpq = mxq(kp, 0, "e4m3")
    notesidx2q = mxq(f64(notes)[:, idx2], 0, "e4m3")
    g0 = kpq.T @ notesidx2q
    gf = np.zeros((I, M))
    gf[:, idx3] = g0
    y = f64(old) * f64(fade) + gf
    return y

@@ -1,0 +1,216 @@
+from contextlib import ExitStack
+
+import concourse.mybir as mybir
+
+D, T, I, J, U, H, M = 512, 2048, 512, 512, 1024, 512, 1024
+FLOPS = 2 * D * H * I + 2 * H * I * J
+
+F32 = mybir.dt.float32
+BF16 = mybir.dt.bfloat16
+I32 = mybir.dt.int32
+U32 = mybir.dt.uint32
+U16 = mybir.dt.uint16
+U8 = mybir.dt.uint8
+FP8X4 = mybir.dt.float8_e4m3fn_x4
+COPY = mybir.ActivationFunctionType.Copy
+MULT = mybir.AluOpType.mult
+ADD = mybir.AluOpType.add
+
+P = 128
+PACK = 4
+ROW_TILES = I // P
+HALF = J // 2
+LIST_COLS = 16
+WK_SPLIT = 80
+
+
+def tile_attend_tab_made_keep_kernel(tc, keys_words, keys_scales, wk, notes, old, fade, offs, offs2, offs3, out):
+    nc = tc.nc
+
+    def entries(list_tile, first, count):
+        return list_tile[:, first // LIST_COLS : (first + count) // LIST_COLS]
+
+    def gather(on_vector, dst, window, offsets):
+        if on_vector:
+            nc.vector.tensor_copy(out=dst, in_=window.indirect(offsets))
+        else:
+            nc.scalar.activation(out=dst, in_=window.indirect(offsets), func=COPY)
+
+    with ExitStack() as ctx:
+        sb = ctx.enter_context(tc.tile_pool(name="sb", bufs=1))
+        psum = ctx.enter_context(tc.psum_pool(name="psum", bufs=1))
+
+        key_list = sb.tile([P, I // LIST_COLS], U16, name="key_list")
+        note_list = sb.tile([P, J // LIST_COLS], U16, name="note_list")
+        place_list = sb.tile([P, J // LIST_COLS], U16, name="place_list")
+
+        pool_scales = sb.tile([P, T], U8, name="pool_scales", align_bytes=64)
+        nc.gpsimd.memset(pool_scales[:].bitcast(I32), 0)
+
+        wk_raw = sb.tile([P, PACK, H], F32, name="wk_raw")
+        nc.sync.dma_start(out=wk_raw[:], in_=wk.rearrange("(p j) h -> p j h", j=PACK))
+        for q in range(4):
+            nc.sync.dma_start(
+                out=pool_scales[32 * q : 32 * q + 4, :].bitcast(I32),
+                in_=keys_scales[0, 4 * q : 4 * q + 4, :].bitcast(I32),
+            )
+        nc.sync.dma_start(key_list[:], offs)
+        pool_words = sb.tile([P, T], I32, name="pool_words", align_bytes=64)
+        nc.sync.dma_start(out=pool_words[:], in_=keys_words[0].rearrange("p t r -> p (t r)").bitcast(I32))
+        nc.sync.dma_start(note_list[:], offs2)
+        note_rows = notes.rearrange("(p t) u -> t p u", t=PACK)
+        planes = []
+        for t in range(PACK):
+            plane = sb.tile([P, U], F32, name="plane%d" % t, tag="plane%d" % t, bufs=1, align_bytes=64)
+            nc.sync.dma_start(out=plane[:], in_=note_rows[t])
+            planes.append(plane)
+        nc.sync.dma_start(place_list[:], offs3)
+        fades = sb.tile([P, ROW_TILES], F32, name="fades")
+        with nc.allow_non_contiguous_dma(reason="one fading factor a partition and row tile"):
+            nc.sync.dma_start(out=fades[:], in_=fade.rearrange("(r p) one -> p (r one)", p=P))
+        olds = []
+        for r in range(ROW_TILES):
+            old_tile = sb.tile([P, M], F32, name="old%d" % r, tag="old%d" % r, bufs=1)
+            nc.sync.dma_start(out=old_tile[:], in_=old[r * P : (r + 1) * P, :])
+            olds.append(old_tile)
+
+        windows = []
+        for r in range(ROW_TILES):
+            window = sb.tile([P, M], F32, name="window%d" % r)
+            (nc.vector if r < 2 else nc.gpsimd).memset(window[:], 0.0)
+            windows.append(window)
+
+        key_scales = sb.tile([P, I], U8, name="key_scales", align_bytes=64)
+        nc.vector.tensor_copy(out=key_scales[:], in_=pool_scales[:].indirect(key_list[:]))
+
+        wk_bf = sb.tile([P, H * PACK], BF16, name="wk_bf", align_bytes=64)
+        wk_dst = wk_bf[:].rearrange("p (t m j) -> p m j t", t=PACK, j=PACK)
+        wk_src = wk_raw[:].rearrange("p j (m t) -> p m j t", t=PACK)
+        nc.scalar.copy(out=wk_dst[:, :WK_SPLIT], in_=wk_src[:, :WK_SPLIT])
+        nc.vector.tensor_copy(out=wk_dst[:, WK_SPLIT:], in_=wk_src[:, WK_SPLIT:])
+        wk_codes = sb.tile([P, H], U32, name="wk_codes", align_bytes=64)
+        wk_scales = sb.tile([P, H], U8, name="wk_scales", align_bytes=64)
+        nc.vector.quantize_mx(out=wk_codes[:].bitcast(FP8X4), scales=wk_scales[:], in_=wk_bf[:])
+
+        key_words = []
+        for r in range(ROW_TILES):
+            words = sb.tile([P, P], U32, name="key_words%d" % r, align_bytes=64)
+            nc.vector.tensor_copy(out=words[:], in_=pool_words[:].bitcast(U32).indirect(entries(key_list, r * P, P)))
+            key_words.append(words)
+
+        kp_banks = []
+        for r in range(ROW_TILES):
+            bank = psum.tile([P, PACK * P], F32, name="kp_bank%d" % r, tag="bank%d" % r)
+            for t in range(PACK):
+                cols = slice(t * P, (t + 1) * P)
+                nc.tensor.matmul_mx(
+                    out=bank[:, cols],
+                    lhsT=wk_codes[:, cols].bitcast(FP8X4),
+                    lhsT_scale=wk_scales[:, cols],
+                    rhs=key_words[r][:].bitcast(FP8X4),
+                    rhs_scale=key_scales[:, r * P : (r + 1) * P],
+                    start=True,
+                    stop=True,
+                )
+            kp_banks.append(bank)
+
+        def round_kp(r, dst):
+            nc.scalar.copy(out=dst, in_=kp_banks[r][:].rearrange("p (t i) -> p i t", t=PACK))
+
+        kp_codes, kp_scales = [], []
+
+        def quantise_kp(rounded, tiles, tag):
+            first = len(kp_codes)
+            codes = sb.tile([P, tiles * P], U32, name="kp_codes%d" % first, tag=tag, bufs=1, align_bytes=64)
+            scales = sb.tile([P, tiles * P], U8, name="kp_scales%d" % first, align_bytes=64)
+            nc.vector.quantize_mx(
+                out=codes[:].bitcast(FP8X4), scales=scales[:], in_=rounded[:].rearrange("p r i t -> p (r i t)")
+            )
+            for r in range(tiles):
+                kp_codes.append(codes[:, r * P : (r + 1) * P])
+                kp_scales.append(scales[:, r * P : (r + 1) * P])
+
+        kp_first = sb.tile([P, 2, P, PACK], BF16, name="kp_first", align_bytes=64)
+        kp_third = sb.tile([P, 1, P, PACK], BF16, name="kp_third", align_bytes=64)
+        round_kp(0, kp_first[:, 0])
+        round_kp(1, kp_first[:, 1])
+        round_kp(2, kp_third[:, 0])
+
+        picked = [sb.tile([P, PACK, HALF], BF16, name="picked%d" % h, tag="picked%d" % h, bufs=1, align_bytes=64) for h in range(2)]
+
+        def gather_plane(t, h, on_vector):
+            gather(on_vector, picked[h][:, t, :], planes[t][:], entries(note_list, h * HALF, HALF))
+
+        for h in range(2):
+            gather_plane(0, h, True)
+        quantise_kp(kp_first, 2, "plane0")
+        for t in (1, 2):
+            for h in range(2):
+                gather_plane(t, h, t == 2)
+        gather_plane(3, 0, False)
+        gather_plane(3, 1, True)
+
+        note_codes, note_scales = [], []
+        for h in range(2):
+            woven = sb.tile([P, HALF, PACK], BF16, name="woven%d" % h, align_bytes=64)
+            dst = woven[:].rearrange("p (c e) t -> p c t e", e=PACK)
+            src = picked[h][:].rearrange("p t (c e) -> p c t e", e=PACK)
+            if h == 0:
+                nc.vector.tensor_copy(out=dst, in_=src)
+            else:
+                nc.scalar.copy(out=dst, in_=src)
+            codes = sb.tile([P, HALF], U32, name="note_codes%d" % h, align_bytes=64)
+            scales = sb.tile([P, HALF], U8, name="note_scales%d" % h, align_bytes=64)
+            nc.vector.quantize_mx(
+                out=codes[:].bitcast(FP8X4), scales=scales[:], in_=woven[:].rearrange("p j t -> p (j t)")
+            )
+            note_codes.append(codes)
+            note_scales.append(scales)
+
+        def place(r, h, on_vector, tag, bufs):
+            bank = psum.tile([P, HALF], F32, name="g0_bank%d_%d" % (r, h), tag="bank%d" % (r + ROW_TILES * (1 - h)))
+            nc.tensor.matmul_mx(
+                out=bank[:],
+                lhsT=kp_codes[r].bitcast(FP8X4),
+                lhsT_scale=kp_scales[r],
+                rhs=note_codes[h][:].bitcast(FP8X4),
+                rhs_scale=note_scales[h][:],
+                start=True,
+                stop=True,
+            )
+            table = sb.tile([P, HALF], F32, name="table%d_%d" % (r, h), tag=tag, bufs=bufs)
+            target = windows[r][:].indirect(entries(place_list, h * HALF, HALF))
+            if on_vector:
+                nc.vector.tensor_copy(out=table[:], in_=bank[:])
+                nc.vector.tensor_copy(out=target, in_=table[:])
+            else:
+                nc.scalar.copy(out=table[:], in_=bank[:])
+                nc.scalar.activation(out=target, in_=table[:], func=COPY)
+
+        def finish(r, pieces, tag):
+            width = M // pieces
+            result = sb.tile([P, M], F32, name="result%d" % r, tag=tag, bufs=1)
+            for c in range(pieces):
+                cols = slice(c * width, (c + 1) * width)
+                nc.vector.scalar_tensor_tensor(
+                    out=result[:, cols], in0=olds[r][:, cols], scalar=fades[:, r : r + 1], in1=windows[r][:, cols],
+                    op0=MULT, op1=ADD,
+                )
+                nc.sync.dma_start(out=out[r * P : (r + 1) * P, cols], in_=result[:, cols])
+
+        place(0, 0, False, "ring_s", 2)
+        place(1, 0, True, "ring_v", 2)
+        kp_last = sb.tile([P, 1, P, PACK], BF16, name="kp_last", tag="plane3", bufs=1, align_bytes=64)
+        round_kp(3, kp_last[:, 0])
+        quantise_kp(kp_third, 1, "picked0")
+        quantise_kp(kp_last, 1, "kp_codes3")
+        place(1, 1, False, "ring_s", 2)
+        place(0, 1, True, "ring_v", 2)
+        place(2, 0, False, "ring_s", 2)
+        finish(0, 1, "result0")
+        finish(1, 1, "result1")
+        place(3, 0, False, "ring_s", 2)
+        place(2, 1, True, "old1", 1)
+        place(3, 1, False, "ring_s", 2)
+        finish(2, 1, "result2")
+        finish(3, 2, "old2")

@@ -21,7 +21,6 @@ PACK = 4
 ROW_TILES = I // P
 HALF = J // 2
 LIST_COLS = 16
-WK_SPLIT = 80
 
 
 def tile_attend_tab_made_keep_kernel(tc, keys_words, keys_scales, wk, notes, old, fade, offs, offs2, offs3, out):
@@ -58,7 +57,7 @@ def tile_attend_tab_made_keep_kernel(tc, keys_words, keys_scales, wk, notes, old
         pool_words = sb.tile([P, T], I32, name="pool_words", align_bytes=64)
         nc.sync.dma_start(out=pool_words[:], in_=keys_words[0].rearrange("p t r -> p (t r)").bitcast(I32))
         nc.sync.dma_start(note_list[:], offs2)
-        note_rows = notes.rearrange("(p t) u -> t p u", t=PACK)
+        note_rows = notes.rearrange("(b t q) u -> t b q u", t=PACK, q=8)
         planes = []
         for t in range(PACK):
             plane = sb.tile([P, U], F32, name="plane%d" % t, tag="plane%d" % t, bufs=1, align_bytes=64)
@@ -77,26 +76,38 @@ def tile_attend_tab_made_keep_kernel(tc, keys_words, keys_scales, wk, notes, old
         windows = []
         for r in range(ROW_TILES):
             window = sb.tile([P, M], F32, name="window%d" % r)
-            (nc.vector if r < 2 else nc.gpsimd).memset(window[:], 0.0)
+            (nc.vector if r < 3 else nc.gpsimd).memset(window[:], 0.0)
             windows.append(window)
 
         key_scales = sb.tile([P, I], U8, name="key_scales", align_bytes=64)
         nc.vector.tensor_copy(out=key_scales[:], in_=pool_scales[:].indirect(key_list[:]))
 
         wk_bf = sb.tile([P, H * PACK], BF16, name="wk_bf", align_bytes=64)
-        wk_dst = wk_bf[:].rearrange("p (t m j) -> p m j t", t=PACK, j=PACK)
-        wk_src = wk_raw[:].rearrange("p j (m t) -> p m j t", t=PACK)
-        nc.scalar.copy(out=wk_dst[:, :WK_SPLIT], in_=wk_src[:, :WK_SPLIT])
-        nc.vector.tensor_copy(out=wk_dst[:, WK_SPLIT:], in_=wk_src[:, WK_SPLIT:])
+        wk_dst = wk_bf[:].rearrange("p (t b g e j) -> p t b g j e", t=PACK, g=2, e=PACK, j=PACK)
+        wk_src = wk_raw[:].rearrange("p j (b t g e) -> p t b g j e", t=PACK, g=2, e=PACK)
+        for t in range(PACK):
+            if t > 0:
+                nc.scalar.copy(out=wk_dst[:, t], in_=wk_src[:, t])
+            else:
+                nc.vector.tensor_copy(out=wk_dst[:, t], in_=wk_src[:, t])
         wk_codes = sb.tile([P, H], U32, name="wk_codes", align_bytes=64)
         wk_scales = sb.tile([P, H], U8, name="wk_scales", align_bytes=64)
-        nc.vector.quantize_mx(out=wk_codes[:].bitcast(FP8X4), scales=wk_scales[:], in_=wk_bf[:])
+        for first in (0, H // 2):
+            cols = slice(first, first + H // 2)
+            nc.vector.quantize_mx(
+                out=wk_codes[:, cols].bitcast(FP8X4),
+                scales=wk_scales[:, cols],
+                in_=wk_bf[:, first * PACK : (first + H // 2) * PACK],
+            )
 
         key_words = []
-        for r in range(ROW_TILES):
-            words = sb.tile([P, P], U32, name="key_words%d" % r, align_bytes=64)
-            nc.vector.tensor_copy(out=words[:], in_=pool_words[:].bitcast(U32).indirect(entries(key_list, r * P, P)))
-            key_words.append(words)
+        for tiles in (1, 1, 2):
+            first = len(key_words)
+            words = sb.tile([P, tiles * P], U32, name="key_words%d" % first, align_bytes=64)
+            nc.vector.tensor_copy(
+                out=words[:], in_=pool_words[:].bitcast(U32).indirect(entries(key_list, first * P, tiles * P))
+            )
+            key_words.extend(words[:, r * P : (r + 1) * P] for r in range(tiles))
 
         kp_banks = []
         for r in range(ROW_TILES):
@@ -107,7 +118,7 @@ def tile_attend_tab_made_keep_kernel(tc, keys_words, keys_scales, wk, notes, old
                     out=bank[:, cols],
                     lhsT=wk_codes[:, cols].bitcast(FP8X4),
                     lhsT_scale=wk_scales[:, cols],
-                    rhs=key_words[r][:].bitcast(FP8X4),
+                    rhs=key_words[r].bitcast(FP8X4),
                     rhs_scale=key_scales[:, r * P : (r + 1) * P],
                     start=True,
                     stop=True,
@@ -136,25 +147,23 @@ def tile_attend_tab_made_keep_kernel(tc, keys_words, keys_scales, wk, notes, old
         round_kp(1, kp_first[:, 1])
         round_kp(2, kp_third[:, 0])
 
-        picked = [sb.tile([P, PACK, HALF], BF16, name="picked%d" % h, tag="picked%d" % h, bufs=1, align_bytes=64) for h in range(2)]
+        picked = sb.tile([P, PACK, J], BF16, name="picked", tag="picked", bufs=1, align_bytes=64)
 
-        def gather_plane(t, h, on_vector):
-            gather(on_vector, picked[h][:, t, :], planes[t][:], entries(note_list, h * HALF, HALF))
+        def gather_plane(t, first, count, on_vector):
+            gather(on_vector, picked[:, t, first : first + count], planes[t][:], entries(note_list, first, count))
 
-        for h in range(2):
-            gather_plane(0, h, True)
+        gather_plane(0, 0, J, True)
         quantise_kp(kp_first, 2, "plane0")
-        for t in (1, 2):
-            for h in range(2):
-                gather_plane(t, h, t == 2)
-        gather_plane(3, 0, False)
-        gather_plane(3, 1, True)
+        gather_plane(1, 0, J, False)
+        gather_plane(2, 0, J, True)
+        gather_plane(3, 0, HALF, False)
+        gather_plane(3, HALF, HALF, True)
 
         note_codes, note_scales = [], []
         for h in range(2):
             woven = sb.tile([P, HALF, PACK], BF16, name="woven%d" % h, align_bytes=64)
             dst = woven[:].rearrange("p (c e) t -> p c t e", e=PACK)
-            src = picked[h][:].rearrange("p t (c e) -> p c t e", e=PACK)
+            src = picked[:, :, h * HALF : (h + 1) * HALF].rearrange("p t (c e) -> p c t e", e=PACK)
             if h == 0:
                 nc.vector.tensor_copy(out=dst, in_=src)
             else:
@@ -167,25 +176,29 @@ def tile_attend_tab_made_keep_kernel(tc, keys_words, keys_scales, wk, notes, old
             note_codes.append(codes)
             note_scales.append(scales)
 
-        def place(r, h, on_vector, tag, bufs):
-            bank = psum.tile([P, HALF], F32, name="g0_bank%d_%d" % (r, h), tag="bank%d" % (r + ROW_TILES * (1 - h)))
-            nc.tensor.matmul_mx(
-                out=bank[:],
-                lhsT=kp_codes[r].bitcast(FP8X4),
-                lhsT_scale=kp_scales[r],
-                rhs=note_codes[h][:].bitcast(FP8X4),
-                rhs_scale=note_scales[h][:],
-                start=True,
-                stop=True,
-            )
-            table = sb.tile([P, HALF], F32, name="table%d_%d" % (r, h), tag=tag, bufs=bufs)
-            target = windows[r][:].indirect(entries(place_list, h * HALF, HALF))
+        def place(r, halves, bank_tag, on_vector, tag, bufs):
+            width = len(halves) * HALF
+            bank = psum.tile([P, width], F32, name="g0_bank%d_%d" % (r, halves[0]), tag=bank_tag)
+            for n, h in enumerate(halves):
+                nc.tensor.matmul_mx(
+                    out=bank[:, n * HALF : (n + 1) * HALF],
+                    lhsT=kp_codes[r].bitcast(FP8X4),
+                    lhsT_scale=kp_scales[r],
+                    rhs=note_codes[h][:].bitcast(FP8X4),
+                    rhs_scale=note_scales[h][:],
+                    start=True,
+                    stop=True,
+                )
+            table = sb.tile([P, width], F32, name="table%d_%d" % (r, halves[0]), tag=tag, bufs=bufs)
             if on_vector:
                 nc.vector.tensor_copy(out=table[:], in_=bank[:])
+                target = windows[r][:].indirect(entries(place_list, halves[0] * HALF, width))
                 nc.vector.tensor_copy(out=target, in_=table[:])
             else:
                 nc.scalar.copy(out=table[:], in_=bank[:])
-                nc.scalar.activation(out=target, in_=table[:], func=COPY)
+                for n, h in enumerate(halves):
+                    target = windows[r][:].indirect(entries(place_list, h * HALF, HALF))
+                    nc.scalar.activation(out=target, in_=table[:, n * HALF : (n + 1) * HALF], func=COPY)
 
         def finish(r, pieces, tag):
             width = M // pieces
@@ -198,19 +211,17 @@ def tile_attend_tab_made_keep_kernel(tc, keys_words, keys_scales, wk, notes, old
                 )
                 nc.sync.dma_start(out=out[r * P : (r + 1) * P, cols], in_=result[:, cols])
 
-        place(0, 0, False, "ring_s", 2)
-        place(1, 0, True, "ring_v", 2)
         kp_last = sb.tile([P, 1, P, PACK], BF16, name="kp_last", tag="plane3", bufs=1, align_bytes=64)
         round_kp(3, kp_last[:, 0])
-        quantise_kp(kp_third, 1, "picked0")
+        quantise_kp(kp_third, 1, "picked")
         quantise_kp(kp_last, 1, "kp_codes3")
-        place(1, 1, False, "ring_s", 2)
-        place(0, 1, True, "ring_v", 2)
-        place(2, 0, False, "ring_s", 2)
+        place(0, (0,), "bank4", False, "ring_s", 2)
+        place(1, (0, 1), "bank5", True, "table1", 1)
+        place(0, (1,), "bank6", False, "ring_s", 2)
+        place(2, (0,), "bank7", False, "ring_s", 2)
         finish(0, 1, "result0")
         finish(1, 1, "result1")
-        place(3, 0, False, "ring_s", 2)
-        place(2, 1, True, "old1", 1)
-        place(3, 1, False, "ring_s", 2)
+        place(2, (1,), "bank0", True, "old1", 1)
+        place(3, (0, 1), "bank1", False, "ring_s", 2)
         finish(2, 1, "result2")
         finish(3, 2, "old2")

@@ -21,6 +21,7 @@ PACK = 4
 ROW_TILES = I // P
 HALF = J // 2
 LIST_COLS = 16
+WK_SPLIT = 80
 
 
 def tile_attend_tab_made_keep_kernel(tc, keys_words, keys_scales, wk, notes, old, fade, offs, offs2, offs3, out):
@@ -57,7 +58,7 @@ def tile_attend_tab_made_keep_kernel(tc, keys_words, keys_scales, wk, notes, old
         pool_words = sb.tile([P, T], I32, name="pool_words", align_bytes=64)
         nc.sync.dma_start(out=pool_words[:], in_=keys_words[0].rearrange("p t r -> p (t r)").bitcast(I32))
         nc.sync.dma_start(note_list[:], offs2)
-        note_rows = notes.rearrange("(b t q) u -> t b q u", t=PACK, q=8)
+        note_rows = notes.rearrange("(p t) u -> t p u", t=PACK)
         planes = []
         for t in range(PACK):
             plane = sb.tile([P, U], F32, name="plane%d" % t, tag="plane%d" % t, bufs=1, align_bytes=64)
@@ -83,22 +84,13 @@ def tile_attend_tab_made_keep_kernel(tc, keys_words, keys_scales, wk, notes, old
         nc.vector.tensor_copy(out=key_scales[:], in_=pool_scales[:].indirect(key_list[:]))
 
         wk_bf = sb.tile([P, H * PACK], BF16, name="wk_bf", align_bytes=64)
-        wk_dst = wk_bf[:].rearrange("p (t b g e j) -> p t b g j e", t=PACK, g=2, e=PACK, j=PACK)
-        wk_src = wk_raw[:].rearrange("p j (b t g e) -> p t b g j e", t=PACK, g=2, e=PACK)
-        for t in range(PACK):
-            if t > 0:
-                nc.scalar.copy(out=wk_dst[:, t], in_=wk_src[:, t])
-            else:
-                nc.vector.tensor_copy(out=wk_dst[:, t], in_=wk_src[:, t])
+        wk_dst = wk_bf[:].rearrange("p (t m j) -> p m j t", t=PACK, j=PACK)
+        wk_src = wk_raw[:].rearrange("p j (m t) -> p m j t", t=PACK)
+        nc.scalar.copy(out=wk_dst[:, :WK_SPLIT], in_=wk_src[:, :WK_SPLIT])
+        nc.vector.tensor_copy(out=wk_dst[:, WK_SPLIT:], in_=wk_src[:, WK_SPLIT:])
         wk_codes = sb.tile([P, H], U32, name="wk_codes", align_bytes=64)
         wk_scales = sb.tile([P, H], U8, name="wk_scales", align_bytes=64)
-        for first in (0, H // 2):
-            cols = slice(first, first + H // 2)
-            nc.vector.quantize_mx(
-                out=wk_codes[:, cols].bitcast(FP8X4),
-                scales=wk_scales[:, cols],
-                in_=wk_bf[:, first * PACK : (first + H // 2) * PACK],
-            )
+        nc.vector.quantize_mx(out=wk_codes[:].bitcast(FP8X4), scales=wk_scales[:], in_=wk_bf[:])
 
         key_words = []
         for tiles in (1, 1, 2):
@@ -200,11 +192,12 @@ def tile_attend_tab_made_keep_kernel(tc, keys_words, keys_scales, wk, notes, old
                     target = windows[r][:].indirect(entries(place_list, h * HALF, HALF))
                     nc.scalar.activation(out=target, in_=table[:, n * HALF : (n + 1) * HALF], func=COPY)
 
-        def finish(r, pieces, tag):
-            width = M // pieces
+        def finish(r, widths, tag):
             result = sb.tile([P, M], F32, name="result%d" % r, tag=tag, bufs=1)
-            for c in range(pieces):
-                cols = slice(c * width, (c + 1) * width)
+            first = 0
+            for width in widths:
+                cols = slice(first, first + width)
+                first += width
                 nc.vector.scalar_tensor_tensor(
                     out=result[:, cols], in0=olds[r][:, cols], scalar=fades[:, r : r + 1], in1=windows[r][:, cols],
                     op0=MULT, op1=ADD,
@@ -219,9 +212,9 @@ def tile_attend_tab_made_keep_kernel(tc, keys_words, keys_scales, wk, notes, old
         place(1, (0, 1), "bank5", True, "table1", 1)
         place(0, (1,), "bank6", False, "ring_s", 2)
         place(2, (0,), "bank7", False, "ring_s", 2)
-        finish(0, 1, "result0")
-        finish(1, 1, "result1")
-        place(2, (1,), "bank0", True, "old1", 1)
+        finish(0, (M,), "result0")
+        finish(1, (M,), "result1")
+        place(2, (1,), "bank0", True, "old0", 1)
         place(3, (0, 1), "bank1", False, "ring_s", 2)
-        finish(2, 1, "result2")
-        finish(3, 2, "old2")
+        finish(2, (M,), "result2")
+        finish(3, (M // 2, M // 4, M // 4), "old2")

@@ -22,6 +22,7 @@ ROW_TILES = I // P
 HALF = J // 2
 LIST_COLS = 16
 WK_SPLIT = 80
+LAST_SPLIT = 320
 
 
 def tile_attend_tab_made_keep_kernel(tc, keys_words, keys_scales, wk, notes, old, fade, offs, offs2, offs3, out):
@@ -45,7 +46,7 @@ def tile_attend_tab_made_keep_kernel(tc, keys_words, keys_scales, wk, notes, old
         place_list = sb.tile([P, J // LIST_COLS], U16, name="place_list")
 
         pool_scales = sb.tile([P, T], U8, name="pool_scales", align_bytes=64)
-        nc.gpsimd.memset(pool_scales[:].bitcast(I32), 0)
+        nc.vector.memset(pool_scales[:].bitcast(I32), 0)
 
         wk_raw = sb.tile([P, PACK, H], F32, name="wk_raw")
         nc.sync.dma_start(out=wk_raw[:], in_=wk.rearrange("(p j) h -> p j h", j=PACK))
@@ -77,7 +78,7 @@ def tile_attend_tab_made_keep_kernel(tc, keys_words, keys_scales, wk, notes, old
         windows = []
         for r in range(ROW_TILES):
             window = sb.tile([P, M], F32, name="window%d" % r)
-            (nc.vector if r < 3 else nc.gpsimd).memset(window[:], 0.0)
+            nc.vector.memset(window[:], 0.0)
             windows.append(window)
 
         key_scales = sb.tile([P, I], U8, name="key_scales", align_bytes=64)
@@ -168,9 +169,8 @@ def tile_attend_tab_made_keep_kernel(tc, keys_words, keys_scales, wk, notes, old
             note_codes.append(codes)
             note_scales.append(scales)
 
-        def place(r, halves, bank_tag, on_vector, tag, bufs):
-            width = len(halves) * HALF
-            bank = psum.tile([P, width], F32, name="g0_bank%d_%d" % (r, halves[0]), tag=bank_tag)
+        def multiply(r, halves, bank_tag):
+            bank = psum.tile([P, len(halves) * HALF], F32, name="g0_bank%d_%d" % (r, halves[0]), tag=bank_tag)
             for n, h in enumerate(halves):
                 nc.tensor.matmul_mx(
                     out=bank[:, n * HALF : (n + 1) * HALF],
@@ -181,16 +181,20 @@ def tile_attend_tab_made_keep_kernel(tc, keys_words, keys_scales, wk, notes, old
                     start=True,
                     stop=True,
                 )
-            table = sb.tile([P, width], F32, name="table%d_%d" % (r, halves[0]), tag=tag, bufs=bufs)
+            return bank
+
+        def place(r, sums, first, on_vector, tag):
+            width = sums.shape[1]
+            table = sb.tile([P, width], F32, name="table%d_%d" % (r, first), tag=tag, bufs=1)
             if on_vector:
-                nc.vector.tensor_copy(out=table[:], in_=bank[:])
-                target = windows[r][:].indirect(entries(place_list, halves[0] * HALF, width))
-                nc.vector.tensor_copy(out=target, in_=table[:])
+                nc.vector.tensor_copy(out=table[:], in_=sums)
+                nc.vector.tensor_copy(out=windows[r][:].indirect(entries(place_list, first, width)), in_=table[:])
             else:
-                nc.scalar.copy(out=table[:], in_=bank[:])
-                for n, h in enumerate(halves):
-                    target = windows[r][:].indirect(entries(place_list, h * HALF, HALF))
-                    nc.scalar.activation(out=target, in_=table[:, n * HALF : (n + 1) * HALF], func=COPY)
+                nc.scalar.copy(out=table[:], in_=sums)
+                for start in range(0, width, HALF):
+                    count = min(HALF, width - start)
+                    target = windows[r][:].indirect(entries(place_list, first + start, count))
+                    nc.scalar.activation(out=target, in_=table[:, start : start + count], func=COPY)
 
         def finish(r, widths, tag):
             result = sb.tile([P, M], F32, name="result%d" % r, tag=tag, bufs=1)
@@ -208,13 +212,18 @@ def tile_attend_tab_made_keep_kernel(tc, keys_words, keys_scales, wk, notes, old
         round_kp(3, kp_last[:, 0])
         quantise_kp(kp_third, 1, "picked")
         quantise_kp(kp_last, 1, "kp_codes3")
-        place(0, (0,), "bank4", False, "ring_s", 2)
-        place(1, (0, 1), "bank5", True, "table1", 1)
-        place(0, (1,), "bank6", False, "ring_s", 2)
-        place(2, (0,), "bank7", False, "ring_s", 2)
-        finish(0, (M,), "result0")
+        faded = sb.tile([P, M], F32, name="faded", tag="plane3", bufs=1, align_bytes=64)
+        nc.gpsimd.tensor_scalar(out=faded[:], in0=olds[0][:], scalar1=fades[:, 0:1], scalar2=0.0, op0=MULT, op1=ADD)
+        place(0, multiply(0, (0,), "bank4")[:], 0, False, "table_a")
+        place(1, multiply(1, (0, 1), "bank5")[:], 0, True, "table_c")
+        place(0, multiply(0, (1,), "bank6")[:], HALF, False, "table_b")
+        place(2, multiply(2, (0, 1), "bank7")[:], 0, False, "table_a")
+        last_sums = multiply(3, (0, 1), "bank0")
+        place(3, last_sums[:, :LAST_SPLIT], 0, True, "table_d")
+        place(3, last_sums[:, LAST_SPLIT:], LAST_SPLIT, False, "table_a")
+        result = sb.tile([P, M], F32, name="result0")
+        nc.gpsimd.tensor_tensor(out=result[:], in0=faded[:], in1=windows[0][:], op=ADD)
+        nc.sync.dma_start(out=out[0:P, :], in_=result[:])
         finish(1, (M,), "result1")
-        place(2, (1,), "bank0", True, "old0", 1)
-        place(3, (0, 1), "bank1", False, "ring_s", 2)
         finish(2, (M,), "result2")
-        finish(3, (M // 2, M // 4, M // 4), "old2")
+        finish(3, (M // 2, M // 2), "old2")

from contextlib import ExitStack

import concourse.mybir as mybir

D, T, I, J, U, H, M = 512, 2048, 512, 512, 1024, 512, 1024
FLOPS = 2 * D * H * I + 2 * H * I * J

F32 = mybir.dt.float32
BF16 = mybir.dt.bfloat16
I32 = mybir.dt.int32
U32 = mybir.dt.uint32
U16 = mybir.dt.uint16
U8 = mybir.dt.uint8
FP8X4 = mybir.dt.float8_e4m3fn_x4
COPY = mybir.ActivationFunctionType.Copy
MULT = mybir.AluOpType.mult
ADD = mybir.AluOpType.add

P = 128
PACK = 4
ROW_TILES = I // P
HALF = J // 2
LIST_COLS = 16
WK_SPLIT = 80
LAST_SPLIT = 320


def tile_attend_tab_made_keep_kernel(tc, keys_words, keys_scales, wk, notes, old, fade, offs, offs2, offs3, out):
    nc = tc.nc

    def entries(list_tile, first, count):
        return list_tile[:, first // LIST_COLS : (first + count) // LIST_COLS]

    def gather(on_vector, dst, window, offsets):
        if on_vector:
            nc.vector.tensor_copy(out=dst, in_=window.indirect(offsets))
        else:
            nc.scalar.activation(out=dst, in_=window.indirect(offsets), func=COPY)

    with ExitStack() as ctx:
        sb = ctx.enter_context(tc.tile_pool(name="sb", bufs=1))
        psum = ctx.enter_context(tc.psum_pool(name="psum", bufs=1))

        key_list = sb.tile([P, I // LIST_COLS], U16, name="key_list")
        note_list = sb.tile([P, J // LIST_COLS], U16, name="note_list")
        place_list = sb.tile([P, J // LIST_COLS], U16, name="place_list")

        pool_scales = sb.tile([P, T], U8, name="pool_scales", align_bytes=64)
        nc.vector.memset(pool_scales[:].bitcast(I32), 0)

        wk_raw = sb.tile([P, PACK, H], F32, name="wk_raw")
        nc.sync.dma_start(out=wk_raw[:], in_=wk.rearrange("(p j) h -> p j h", j=PACK))
        for q in range(4):
            nc.sync.dma_start(
                out=pool_scales[32 * q : 32 * q + 4, :].bitcast(I32),
                in_=keys_scales[0, 4 * q : 4 * q + 4, :].bitcast(I32),
            )
        nc.sync.dma_start(key_list[:], offs)
        pool_words = sb.tile([P, T], I32, name="pool_words", align_bytes=64)
        nc.sync.dma_start(out=pool_words[:], in_=keys_words[0].rearrange("p t r -> p (t r)").bitcast(I32))
        nc.sync.dma_start(note_list[:], offs2)
        note_rows = notes.rearrange("(p t) u -> t p u", t=PACK)
        planes = []
        for t in range(PACK):
            plane = sb.tile([P, U], F32, name="plane%d" % t, tag="plane%d" % t, bufs=1, align_bytes=64)
            nc.sync.dma_start(out=plane[:], in_=note_rows[t])
            planes.append(plane)
        nc.sync.dma_start(place_list[:], offs3)
        fades = sb.tile([P, ROW_TILES], F32, name="fades")
        with nc.allow_non_contiguous_dma(reason="one fading factor a partition and row tile"):
            nc.sync.dma_start(out=fades[:], in_=fade.rearrange("(r p) one -> p (r one)", p=P))
        olds = []
        for r in range(ROW_TILES):
            old_tile = sb.tile([P, M], F32, name="old%d" % r, tag="old%d" % r, bufs=1)
            nc.sync.dma_start(out=old_tile[:], in_=old[r * P : (r + 1) * P, :])
            olds.append(old_tile)

        windows = []
        for r in range(ROW_TILES):
            window = sb.tile([P, M], F32, name="window%d" % r)
            nc.vector.memset(window[:], 0.0)
            windows.append(window)

        key_scales = sb.tile([P, I], U8, name="key_scales", align_bytes=64)
        nc.vector.tensor_copy(out=key_scales[:], in_=pool_scales[:].indirect(key_list[:]))

        wk_bf = sb.tile([P, H * PACK], BF16, name="wk_bf", align_bytes=64)
        wk_dst = wk_bf[:].rearrange("p (t m j) -> p m j t", t=PACK, j=PACK)
        wk_src = wk_raw[:].rearrange("p j (m t) -> p m j t", t=PACK)
        nc.scalar.copy(out=wk_dst[:, :WK_SPLIT], in_=wk_src[:, :WK_SPLIT])
        nc.vector.tensor_copy(out=wk_dst[:, WK_SPLIT:], in_=wk_src[:, WK_SPLIT:])
        wk_codes = sb.tile([P, H], U32, name="wk_codes", align_bytes=64)
        wk_scales = sb.tile([P, H], U8, name="wk_scales", align_bytes=64)
        nc.vector.quantize_mx(out=wk_codes[:].bitcast(FP8X4), scales=wk_scales[:], in_=wk_bf[:])

        key_words = []
        for tiles in (1, 1, 2):
            first = len(key_words)
            words = sb.tile([P, tiles * P], U32, name="key_words%d" % first, align_bytes=64)
            nc.vector.tensor_copy(
                out=words[:], in_=pool_words[:].bitcast(U32).indirect(entries(key_list, first * P, tiles * P))
            )
            key_words.extend(words[:, r * P : (r + 1) * P] for r in range(tiles))

        kp_banks = []
        for r in range(ROW_TILES):
            bank = psum.tile([P, PACK * P], F32, name="kp_bank%d" % r, tag="bank%d" % r)
            for t in range(PACK):
                cols = slice(t * P, (t + 1) * P)
                nc.tensor.matmul_mx(
                    out=bank[:, cols],
                    lhsT=wk_codes[:, cols].bitcast(FP8X4),
                    lhsT_scale=wk_scales[:, cols],
                    rhs=key_words[r].bitcast(FP8X4),
                    rhs_scale=key_scales[:, r * P : (r + 1) * P],
                    start=True,
                    stop=True,
                )
            kp_banks.append(bank)

        def round_kp(r, dst):
            nc.scalar.copy(out=dst, in_=kp_banks[r][:].rearrange("p (t i) -> p i t", t=PACK))

        kp_codes, kp_scales = [], []

        def quantise_kp(rounded, tiles, tag):
            first = len(kp_codes)
            codes = sb.tile([P, tiles * P], U32, name="kp_codes%d" % first, tag=tag, bufs=1, align_bytes=64)
            scales = sb.tile([P, tiles * P], U8, name="kp_scales%d" % first, align_bytes=64)
            nc.vector.quantize_mx(
                out=codes[:].bitcast(FP8X4), scales=scales[:], in_=rounded[:].rearrange("p r i t -> p (r i t)")
            )
            for r in range(tiles):
                kp_codes.append(codes[:, r * P : (r + 1) * P])
                kp_scales.append(scales[:, r * P : (r + 1) * P])

        kp_first = sb.tile([P, 2, P, PACK], BF16, name="kp_first", align_bytes=64)
        kp_third = sb.tile([P, 1, P, PACK], BF16, name="kp_third", align_bytes=64)
        round_kp(0, kp_first[:, 0])
        round_kp(1, kp_first[:, 1])
        round_kp(2, kp_third[:, 0])

        picked = sb.tile([P, PACK, J], BF16, name="picked", tag="picked", bufs=1, align_bytes=64)

        def gather_plane(t, first, count, on_vector):
            gather(on_vector, picked[:, t, first : first + count], planes[t][:], entries(note_list, first, count))

        gather_plane(0, 0, J, True)
        quantise_kp(kp_first, 2, "plane0")
        gather_plane(1, 0, J, False)
        gather_plane(2, 0, J, True)
        gather_plane(3, 0, HALF, False)
        gather_plane(3, HALF, HALF, True)

        note_codes, note_scales = [], []
        for h in range(2):
            woven = sb.tile([P, HALF, PACK], BF16, name="woven%d" % h, align_bytes=64)
            dst = woven[:].rearrange("p (c e) t -> p c t e", e=PACK)
            src = picked[:, :, h * HALF : (h + 1) * HALF].rearrange("p t (c e) -> p c t e", e=PACK)
            if h == 0:
                nc.vector.tensor_copy(out=dst, in_=src)
            else:
                nc.scalar.copy(out=dst, in_=src)
            codes = sb.tile([P, HALF], U32, name="note_codes%d" % h, align_bytes=64)
            scales = sb.tile([P, HALF], U8, name="note_scales%d" % h, align_bytes=64)
            nc.vector.quantize_mx(
                out=codes[:].bitcast(FP8X4), scales=scales[:], in_=woven[:].rearrange("p j t -> p (j t)")
            )
            note_codes.append(codes)
            note_scales.append(scales)

        def multiply(r, halves, bank_tag):
            bank = psum.tile([P, len(halves) * HALF], F32, name="g0_bank%d_%d" % (r, halves[0]), tag=bank_tag)
            for n, h in enumerate(halves):
                nc.tensor.matmul_mx(
                    out=bank[:, n * HALF : (n + 1) * HALF],
                    lhsT=kp_codes[r].bitcast(FP8X4),
                    lhsT_scale=kp_scales[r],
                    rhs=note_codes[h][:].bitcast(FP8X4),
                    rhs_scale=note_scales[h][:],
                    start=True,
                    stop=True,
                )
            return bank

        def place(r, sums, first, on_vector, tag):
            width = sums.shape[1]
            table = sb.tile([P, width], F32, name="table%d_%d" % (r, first), tag=tag, bufs=1)
            if on_vector:
                nc.vector.tensor_copy(out=table[:], in_=sums)
                nc.vector.tensor_copy(out=windows[r][:].indirect(entries(place_list, first, width)), in_=table[:])
            else:
                nc.scalar.copy(out=table[:], in_=sums)
                for start in range(0, width, HALF):
                    count = min(HALF, width - start)
                    target = windows[r][:].indirect(entries(place_list, first + start, count))
                    nc.scalar.activation(out=target, in_=table[:, start : start + count], func=COPY)

        def finish(r, widths, tag):
            result = sb.tile([P, M], F32, name="result%d" % r, tag=tag, bufs=1)
            first = 0
            for width in widths:
                cols = slice(first, first + width)
                first += width
                nc.vector.scalar_tensor_tensor(
                    out=result[:, cols], in0=olds[r][:, cols], scalar=fades[:, r : r + 1], in1=windows[r][:, cols],
                    op0=MULT, op1=ADD,
                )
                nc.sync.dma_start(out=out[r * P : (r + 1) * P, cols], in_=result[:, cols])

        kp_last = sb.tile([P, 1, P, PACK], BF16, name="kp_last", tag="plane3", bufs=1, align_bytes=64)
        round_kp(3, kp_last[:, 0])
        quantise_kp(kp_third, 1, "picked")
        quantise_kp(kp_last, 1, "kp_codes3")
        faded = sb.tile([P, M], F32, name="faded", tag="plane3", bufs=1, align_bytes=64)
        nc.gpsimd.tensor_scalar(out=faded[:], in0=olds[0][:], scalar1=fades[:, 0:1], scalar2=0.0, op0=MULT, op1=ADD)
        place(0, multiply(0, (0,), "bank4")[:], 0, False, "table_a")
        place(1, multiply(1, (0, 1), "bank5")[:], 0, True, "table_c")
        place(0, multiply(0, (1,), "bank6")[:], HALF, False, "table_b")
        place(2, multiply(2, (0, 1), "bank7")[:], 0, False, "table_a")
        last_sums = multiply(3, (0, 1), "bank0")
        place(3, last_sums[:, :LAST_SPLIT], 0, True, "table_d")
        place(3, last_sums[:, LAST_SPLIT:], LAST_SPLIT, False, "table_a")
        result = sb.tile([P, M], F32, name="result0")
        nc.gpsimd.tensor_tensor(out=result[:], in0=faded[:], in1=windows[0][:], op=ADD)
        nc.sync.dma_start(out=out[0:P, :], in_=result[:])
        finish(1, (M,), "result1")
        finish(2, (M,), "result2")
        finish(3, (M // 2, M // 2), "old2")
